import numpy as np
import ml_dtypes


def mxq(x, axis, fmt="e4m3"):
    dtype, down = {"e4m3": (ml_dtypes.float8_e4m3fn, 7), "e5m2": (ml_dtypes.float8_e5m2, 14)}[fmt]
    v = np.moveaxis(np.asarray(x, np.float32).astype(ml_dtypes.bfloat16).astype(np.float64), axis, -1)
    blocks = v.reshape(v.shape[:-1] + (-1, 32))
    amax = np.abs(blocks).max(-1, keepdims=True)
    byte = np.maximum(np.where(amax > 0, np.frexp(amax)[1] - 1 + 127, 0) - down, 1)
    scale = np.exp2(byte - 127.0)
    codes = (blocks / scale).astype(np.float32).astype(dtype).astype(np.float64)
    return np.moveaxis((codes * scale).reshape(v.shape), -1, axis)


WIDE = False


def mx_kscale(k):
    if not WIDE:
        return np.ones(k)
    levels = np.array([10, -10, 5, -5, 0])
    if k % 512:
        return np.exp2(np.random.permutation(np.resize(levels, k // 32))).repeat(32)
    a = np.empty((k // 512, 16))
    for p in range(k // 512):
        a[p, :8] = np.random.permutation(np.resize(levels, 8))
        for g in range(8):
            far = levels[np.abs(levels - a[p, g]) >= 10]
            a[p, g + 8] = far[np.random.randint(len(far))]
    return np.exp2(a.ravel()).repeat(32)


def f64(x):
    return np.asarray(x).astype(np.float64)


def striped(idx):
    return np.tile(idx.reshape(-1, 16).T, (8, 1)).astype(np.uint16)


def unstriped(offs):
    return offs[:16].T.reshape(-1).astype(np.int64)


E2M1 = np.array([0.0, 0.5, 1.0, 1.5, 2.0, 3.0, 4.0, 6.0, -0.0, -0.5, -1.0, -1.5, -2.0, -3.0, -4.0, -6.0])


def pack_weight(w, fmt):
    k, n = w.shape
    w = f64(np.asarray(w, np.float32).astype(ml_dtypes.bfloat16)).reshape(k // 32, 32, n)
    amax = np.abs(w).max(1)
    if fmt == "e4m3":
        byte = np.frexp(amax)[1] - 1 + 127 - 7
    else:
        mant, ex = np.frexp(amax / 6.0)
        byte = np.where(mant > 0.5, ex, ex - 1) + 127
    byte = np.clip(np.where(amax > 0, byte, 1), 1, 254)
    scaled = (w * np.exp2(127.0 - byte)[:, None, :]).reshape(k, n).astype(np.float32)
    by_word = np.ascontiguousarray(scaled.reshape(k // 512, 128, 4, n).transpose(0, 1, 3, 2))
    if fmt == "e4m3":
        words = by_word.astype(ml_dtypes.float8_e4m3fn).view(np.uint8)
    else:
        c = by_word.astype(ml_dtypes.float4_e2m1fn).view(np.uint8) & 0xF
        words = (c[..., 0::2] | (c[..., 1::2] << 4)).reshape(k // 512, 128, 2 * n)
    return np.ascontiguousarray(words), np.ascontiguousarray(byte.astype(np.uint8).reshape(k // 512, 16, n))


def unpack_weight(words, scales, fmt):
    g, _, n = scales.shape
    words = np.ascontiguousarray(words).reshape(g, 128, n, -1)
    if fmt == "e4m3":
        vals = words.view(ml_dtypes.float8_e4m3fn).astype(np.float64)
    else:
        nib = np.empty((g, 128, n, 4), np.uint8)
        nib[..., 0::2] = words & 0xF
        nib[..., 1::2] = words >> 4
        vals = E2M1[nib]
    vals = vals * np.repeat(np.exp2(scales.astype(np.float64) - 127.0), 8, axis=1)[..., None]
    return vals.transpose(0, 1, 3, 2).reshape(g * 512, n)


def gelu(v):
    return 0.5 * v * (1.0 + np.tanh(np.sqrt(2.0 / np.pi) * (v + 0.044715 * v**3)))


K, T, E, C, N = 1536, 768, 12, 128, 256


def by_expert(wq, xq):
    return np.concatenate([wq[e].T @ xq[:, e * C:(e + 1) * C] for e in range(E)], axis=1)


def setup_inputs():
    n = np.random.standard_normal
    s = mx_kscale(K)[:, None]
    first = np.random.permutation(np.repeat(np.arange(E), T // E))
    second = (first + 1 + np.random.permutation(np.repeat(np.arange(E - 1), -(-T // (E - 1)))[:T])) % E
    while np.bincount(second, minlength=E).max() != T // E:
        load = np.bincount(second, minlength=E); hi, lo = int(load.argmax()), int(load.argmin())
        t = np.flatnonzero((second == hi) & (first != lo))[0]; second[t] = lo
    slot_token = np.empty(E * C, np.int64); pos = np.empty((2, T), np.int64); fill = np.zeros(E, np.int64)
    place = np.stack([np.random.permutation(C) for _ in range(E)])
    for r, deal in enumerate((first, second)):
        for t in np.random.permutation(T):
            e = deal[t]; j = e * C + place[e, fill[e]]; fill[e] += 1; slot_token[j] = t; pos[r, t] = j
    g = np.random.uniform(0.2, 0.8, T)
    x = pack_weight(n((K, T)) * s, "e4m3")
    return {
        "x_words": x[0],
        "x_scales": x[1],
        "w": (n((E + 1, K, N)) / np.sqrt(K) / s[None]).astype(np.float32),
        "b": (0.3 * n((N, E + 1))).astype(np.float32),
        "gate": np.stack([np.tile(g, (N, 1)), np.tile(1.0 - g, (N, 1))]).astype(np.float32),
        "offs": striped(slot_token),
        "pos1": striped(pos[0]),
        "pos2": striped(pos[1]),
    }


def reference(x_words, x_scales, w, b, gate, offs, pos1, pos2):
    idx = unstriped(offs)
    wq = mxq(f64(w), 1, "e4m3")
    xs = unpack_weight(x_words, x_scales, "e4m3")
    ys = gelu((wq[E].T @ xs) + f64(b)[:, E:])
    xq = unpack_weight(x_words, x_scales, "e4m3")[:, idx]
    y = by_expert(wq, xq)
    y = gelu(y + np.repeat(f64(b)[:, :E], C, axis=1))
    return ys + f64(gate[0]) * y[:, unstriped(pos1)] + f64(gate[1]) * y[:, unstriped(pos2)]

@@ -1,0 +1,210 @@
+from contextlib import ExitStack
+
+import concourse.mybir as mybir
+
+K, T, E, C, N = 1536, 768, 12, 128, 256
+S = E * C
+FLOPS = 2 * K * N * (S + T)
+
+F32 = mybir.dt.float32
+BF16 = mybir.dt.bfloat16
+I32 = mybir.dt.int32
+U32 = mybir.dt.uint32
+U16 = mybir.dt.uint16
+U8 = mybir.dt.uint8
+FP8X4 = mybir.dt.float8_e4m3fn_x4
+MULT = mybir.AluOpType.mult
+ADD = mybir.AluOpType.add
+GELU = mybir.ActivationFunctionType.Gelu_apprx_tanh
+
+P = 128
+PACK = 4
+ROWS = P * PACK
+PASSES = K // ROWS
+HALVES = N // P
+GROUP = 2
+LIST = 16
+SPLIT = 0
+WHOLE = E - SPLIT
+SCALAR_ONLY = 0
+VECTOR_TWO = 10
+
+
+def tile_moe_shr_lin_gelu_kernel(
+    tc, x_words, x_scales, w, b, gate, offs, pos1, pos2, out
+):
+    nc = tc.nc
+    with ExitStack() as ctx:
+        keep = ctx.enter_context(tc.tile_pool(name="keep", bufs=1))
+        rawp = ctx.enter_context(tc.tile_pool(name="rawp", bufs=8))
+        rawq = ctx.enter_context(tc.tile_pool(name="rawq", bufs=6))
+        stage = ctx.enter_context(tc.tile_pool(name="stage", bufs=14))
+        tokp = ctx.enter_context(tc.tile_pool(name="tokp", bufs=2))
+        codep = ctx.enter_context(tc.tile_pool(name="codep", bufs=6))
+        psum = ctx.enter_context(tc.psum_pool(name="psum", bufs=2))
+        psum1 = ctx.enter_context(tc.psum_pool(name="psum1", bufs=1))
+
+        offs_t = keep.tile([P, S // LIST], U16, name="offs_t")
+        nc.sync.dma_start(offs_t[:], offs)
+        xs = keep.tile([P, T], U8, name="xs", align_bytes=64)
+        nc.vector.memset(xs[:].bitcast(I32), 0)
+        xw = []
+        for o in range(PASSES):
+            t = keep.tile([P, T], I32, name="xw%d" % o, align_bytes=64)
+            nc.sync.dma_start(t[:], x_words[o].rearrange("p t r -> p (t r)").bitcast(I32))
+            xw.append(t)
+        for q in range(4):
+            nc.sync.dma_start(
+                xs[32 * q : 32 * q + 4 * PASSES, :].bitcast(I32),
+                x_scales[:, 4 * q : 4 * q + 4, :].bitcast(I32),
+            )
+        bias = keep.tile([P, HALVES, E + 1], F32, name="bias")
+        pos = [keep.tile([P, T // LIST], U16, name="pos%d" % r) for r in range(2)]
+        gates = [keep.tile([P, T], F32, name="gate%d" % r) for r in range(2)]
+        y = [keep.tile([P, S], F32, name="y%d" % h) for h in range(HALVES)]
+        ys = [keep.tile([P, T], F32, name="ys%d" % h) for h in range(HALVES)]
+
+        rows = w.rearrange("e (o p j) n -> p (e o) (j n)", p=P, j=PACK)
+
+        def load_run(first, count):
+            raw = rawp.tile([P, count, PACK * N], F32, name="raw")
+            nc.sync.dma_start(raw[:], rows[:, first : first + count, :])
+            return [raw[:, i, :].rearrange("p (j n) -> p j n", j=PACK) for i in range(count)]
+
+        def load_passes(e, cols):
+            raws = []
+            for o in range(PASSES):
+                raw = rawq.tile([P, PACK, cols.stop - cols.start], F32, name="rawpass")
+                nc.sync.dma_start(raw[:], w[e, o * ROWS : (o + 1) * ROWS, cols].rearrange("(p j) n -> p j n", j=PACK))
+                raws.append(raw[:])
+            return raws
+
+        def cast(raw, on_vector, grouped):
+            dst = grouped.rearrange("p (c i) j -> p c j i", i=4)
+            src = raw.rearrange("p j (c i) -> p c j i", i=4)
+            if on_vector:
+                nc.vector.tensor_copy(dst, src)
+            else:
+                nc.scalar.copy(dst, src)
+
+        def quantise(grouped):
+            width = grouped.shape[1]
+            codes = codep.tile([P, width], U32, name="codes", align_bytes=64)
+            scales = codep.tile([P, width], U8, name="scales", align_bytes=64)
+            nc.vector.quantize_mx(
+                out=codes[:].bitcast(FP8X4), scales=scales[:], in_=grouped.rearrange("p n j -> p (n j)")
+            )
+            return codes, scales
+
+        def gather_tokens(g):
+            width = GROUP * C
+            cols = offs_t[:, g * width // LIST : (g + 1) * width // LIST]
+            words = []
+            for o in range(PASSES):
+                t = tokp.tile([P, width], U32, name="gw%d" % o, align_bytes=64)
+                nc.vector.tensor_copy(t[:], xw[o][:].bitcast(U32).indirect(cols))
+                words.append(t)
+            sc = tokp.tile([P, width], U8, name="gs", align_bytes=64)
+            nc.vector.tensor_copy(sc[:], xs[:].indirect(cols))
+            return words, sc
+
+        tokens = {}
+
+        def routed(e, halves, raws, vector_passes):
+            words, sc = tokens[e // GROUP]
+            slots = slice((e % GROUP) * C, (e % GROUP + 1) * C)
+            acc = [psum.tile([P, C], F32, name="acc%d" % h) for h in halves]
+            for o in range(PASSES):
+                grouped = stage.tile([P, len(halves) * P, PACK], BF16, name="grouped", align_bytes=64)
+                cast(raws[o], o in vector_passes, grouped[:])
+                codes, scales = quantise(grouped[:])
+                for i in range(len(halves)):
+                    nc.tensor.matmul_mx(
+                        out=acc[i][:],
+                        lhsT=codes[:, i * P : (i + 1) * P].bitcast(FP8X4),
+                        lhsT_scale=scales[:, i * P : (i + 1) * P],
+                        rhs=words[o][:, slots].bitcast(FP8X4),
+                        rhs_scale=sc[4 * o : P, slots],
+                        start=(o == 0),
+                        stop=(o == PASSES - 1),
+                    )
+            for i, h in enumerate(halves):
+                nc.scalar.activation(y[h][:, e * C : (e + 1) * C], acc[i][:], GELU, bias=bias[:, h, e : e + 1])
+
+        def load_gates():
+            for r in range(2):
+                nc.sync.dma_start(gates[r][:], gate[r, 0:P, :])
+
+        def fetch(h, r, s, name):
+            t = keep.tile([P, s.stop - s.start], F32, name=name, align_bytes=64)
+            nc.vector.tensor_tensor(
+                t[:], y[h][:].indirect(pos[r][:, s.start // LIST : s.stop // LIST]), gates[r][:, s], MULT
+            )
+            return t
+
+        everything = slice(0, N)
+        whole = slice(0, T)
+        last = WHOLE * PASSES
+        cuts = [0, 1] + list(range(2, last - 3, PASSES)) + [last - 2, last - 1, last]
+        landed = []
+        for e in range(WHOLE):
+            while len(landed) < min((e + 1) * PASSES, last):
+                nxt = cuts[cuts.index(len(landed)) + 1]
+                landed.extend(load_run(len(landed), nxt - len(landed)))
+            raws = landed[e * PASSES : (e + 1) * PASSES]
+            if e == 0:
+                nc.sync.dma_start(bias[:], b.rearrange("(h p) e -> p h e", p=P))
+                nc.sync.dma_start(pos[0][:], pos1)
+                nc.sync.dma_start(pos[1][:], pos2)
+            if e % GROUP == 0:
+                tokens[e // GROUP] = gather_tokens(e // GROUP)
+            routed(e, [0, 1], raws, [] if e < SCALAR_ONLY else [2] if e < VECTOR_TWO else [1, 2])
+        for e in range(WHOLE, E):
+            if e % GROUP == 0:
+                tokens[e // GROUP] = gather_tokens(e // GROUP)
+            routed(e, [0], load_passes(e, slice(0, P)), [1, 2])
+        load_gates()
+
+        parts = [slice(0, 512), slice(512, T)]
+        sacc = [
+            [psum1.tile([P, s.stop - s.start], F32, name="sacc%d_%d" % (h, i)) for i, s in enumerate(parts)]
+            for h in range(HALVES)
+        ]
+        raws = load_passes(E, everything)
+
+        def shared_pass(o):
+            grouped = keep.tile([P, N, PACK], BF16, name="hold%d" % o, align_bytes=64)
+            cast(raws[o], False, grouped[:])
+            codes, scales = quantise(grouped[:])
+            for h in range(HALVES):
+                for i, s in enumerate(parts):
+                    nc.tensor.matmul_mx(
+                        out=sacc[h][i][:],
+                        lhsT=codes[:, h * P : (h + 1) * P].bitcast(FP8X4),
+                        lhsT_scale=scales[:, h * P : (h + 1) * P],
+                        rhs=xw[o][:, s].bitcast(FP8X4),
+                        rhs_scale=xs[4 * o : P, s],
+                        start=(o == 0),
+                        stop=(o == PASSES - 1),
+                    )
+
+        def shared_out():
+            for h in range(HALVES):
+                for i, s in enumerate(parts):
+                    nc.scalar.activation(ys[h][:, s], sacc[h][i][:], GELU, bias=bias[:, h, E : E + 1])
+
+        a0 = fetch(0, 0, whole, "a0")
+        b0 = fetch(0, 1, whole, "b0")
+        shared_pass(0)
+        shared_pass(1)
+        a1 = fetch(1, 0, whole, "hold1")
+        shared_pass(2)
+        shared_out()
+        nc.vector.tensor_tensor(a0[:], a0[:], b0[:], ADD)
+        b1 = fetch(1, 1, whole, "hold2")
+        nc.vector.tensor_tensor(b0[:], a0[:], ys[0][:], ADD)
+        nc.sync.dma_start(out[0:P, :], b0[:])
+        nc.vector.tensor_tensor(a1[:], a1[:], b1[:], ADD)
+        for s in (slice(0, 384), slice(384, T)):
+            nc.vector.tensor_tensor(b1[:, s], a1[:, s], ys[1][:, s], ADD)
+            nc.sync.dma_start(out[P : 2 * P, s], b1[:, s])

@@ -1,6 +1,7 @@
 from contextlib import ExitStack
 
 import concourse.mybir as mybir
+from concourse.masks import make_identity
 
 K, T, E, C, N = 1536, 768, 12, 128, 256
 S = E * C
@@ -22,12 +23,13 @@ PACK = 4
 ROWS = P * PACK
 PASSES = K // ROWS
 HALVES = N // P
-GROUP = 2
+GROUP = 4
 LIST = 16
-SPLIT = 0
+SPLIT = 4
 WHOLE = E - SPLIT
-SCALAR_ONLY = 0
-VECTOR_TWO = 10
+BANK = 512
+RUN = 4
+LAST = PASSES - 1
 
 
 def tile_moe_shr_lin_gelu_kernel(
@@ -36,104 +38,145 @@ def tile_moe_shr_lin_gelu_kernel(
     nc = tc.nc
     with ExitStack() as ctx:
         keep = ctx.enter_context(tc.tile_pool(name="keep", bufs=1))
-        rawp = ctx.enter_context(tc.tile_pool(name="rawp", bufs=8))
-        rawq = ctx.enter_context(tc.tile_pool(name="rawq", bufs=6))
-        stage = ctx.enter_context(tc.tile_pool(name="stage", bufs=14))
-        tokp = ctx.enter_context(tc.tile_pool(name="tokp", bufs=2))
-        codep = ctx.enter_context(tc.tile_pool(name="codep", bufs=6))
+        rawp = ctx.enter_context(tc.tile_pool(name="rawp", bufs=9))
+        stage = ctx.enter_context(tc.tile_pool(name="stage", bufs=7))
+        codep = ctx.enter_context(tc.tile_pool(name="codep", bufs=4))
         psum = ctx.enter_context(tc.psum_pool(name="psum", bufs=2))
         psum1 = ctx.enter_context(tc.psum_pool(name="psum1", bufs=1))
 
         offs_t = keep.tile([P, S // LIST], U16, name="offs_t")
         nc.sync.dma_start(offs_t[:], offs)
         xs = keep.tile([P, T], U8, name="xs", align_bytes=64)
-        nc.vector.memset(xs[:].bitcast(I32), 0)
-        xw = []
-        for o in range(PASSES):
-            t = keep.tile([P, T], I32, name="xw%d" % o, align_bytes=64)
-            nc.sync.dma_start(t[:], x_words[o].rearrange("p t r -> p (t r)").bitcast(I32))
-            xw.append(t)
+        nc.gpsimd.memset(xs[:].bitcast(I32), 0)
         for q in range(4):
-            nc.sync.dma_start(
+            nc.scalar.dma_start(
                 xs[32 * q : 32 * q + 4 * PASSES, :].bitcast(I32),
                 x_scales[:, 4 * q : 4 * q + 4, :].bitcast(I32),
             )
+        xw = [keep.tile([P, T], I32, name="xw%d" % o, align_bytes=64) for o in range(PASSES)]
         bias = keep.tile([P, HALVES, E + 1], F32, name="bias")
         pos = [keep.tile([P, T // LIST], U16, name="pos%d" % r) for r in range(2)]
         gates = [keep.tile([P, T], F32, name="gate%d" % r) for r in range(2)]
         y = [keep.tile([P, S], F32, name="y%d" % h) for h in range(HALVES)]
         ys = [keep.tile([P, T], F32, name="ys%d" % h) for h in range(HALVES)]
+        parts = [slice(0, BANK), slice(BANK, T)]
 
         rows = w.rearrange("e (o p j) n -> p (e o) (j n)", p=P, j=PACK)
 
-        def load_run(first, count):
-            raw = rawp.tile([P, count, PACK * N], F32, name="raw")
-            nc.sync.dma_start(raw[:], rows[:, first : first + count, :])
-            return [raw[:, i, :].rearrange("p (j n) -> p j n", j=PACK) for i in range(count)]
+        def load_run(first, count, place=None):
+            if place is None:
+                raw = rawp.tile([P, count, PACK * N], F32, name="raw")
+            else:
+                raw = keep.tile([P, count, PACK * N], F32, name=place, align_bytes=64)
+            step = count if place is None else 1
+            for i in range(0, count, step):
+                nc.sync.dma_start(raw[:, i : i + step, :], rows[:, first + i : first + i + step, :])
+            return raw[:].rearrange("p o (j n) -> p o j n", j=PACK)
 
         def load_passes(e, cols):
-            raws = []
+            raw = rawp.tile([P, PASSES, PACK, cols.stop - cols.start], F32, name="raw")
             for o in range(PASSES):
-                raw = rawq.tile([P, PACK, cols.stop - cols.start], F32, name="rawpass")
-                nc.sync.dma_start(raw[:], w[e, o * ROWS : (o + 1) * ROWS, cols].rearrange("(p j) n -> p j n", j=PACK))
-                raws.append(raw[:])
-            return raws
+                nc.sync.dma_start(
+                    raw[:, o, :, :], w[e, o * ROWS : (o + 1) * ROWS, cols].rearrange("(p j) n -> p j n", j=PACK)
+                )
+            return raw[:]
 
-        def cast(raw, on_vector, grouped):
-            dst = grouped.rearrange("p (c i) j -> p c j i", i=4)
-            src = raw.rearrange("p j (c i) -> p c j i", i=4)
+        def regroup(raw, on_vector, place=None, by_pass=False):
+            count, width = raw.shape[1], raw.shape[3]
+            if place is None:
+                grouped = stage.tile([P, count, width, PACK], BF16, name="grouped", align_bytes=64)
+            else:
+                grouped = keep.tile([P, count, width, PACK], BF16, name=place, align_bytes=64)
+            dst = grouped[:].rearrange("p o (c i) j -> p o c j i", i=RUN)
+            src = raw.rearrange("p o j (c i) -> p o c j i", i=RUN)
             if on_vector:
                 nc.vector.tensor_copy(dst, src)
+            elif by_pass:
+                for o in range(count):
+                    nc.scalar.copy(dst[:, o], src[:, o])
             else:
                 nc.scalar.copy(dst, src)
+            return grouped[:]
 
-        def quantise(grouped):
-            width = grouped.shape[1]
-            codes = codep.tile([P, width], U32, name="codes", align_bytes=64)
-            scales = codep.tile([P, width], U8, name="scales", align_bytes=64)
+        def encode(grouped, held=None):
+            count, width = grouped.shape[1], grouped.shape[2]
+            if held is None:
+                codes = codep.tile([P, count * width], U32, name="codes", align_bytes=64)
+            else:
+                codes = keep.tile([P, count * width], U32, name=held, align_bytes=64)
+            scales = codep.tile([P, count * width], U8, name="scales", align_bytes=64)
             nc.vector.quantize_mx(
-                out=codes[:].bitcast(FP8X4), scales=scales[:], in_=grouped.rearrange("p n j -> p (n j)")
+                out=codes[:].bitcast(FP8X4), scales=scales[:], in_=grouped.rearrange("p o n j -> p (o n j)")
             )
-            return codes, scales
+            return [(codes[:, i * width : (i + 1) * width], scales[:, i * width : (i + 1) * width]) for i in range(count)]
+
+        def quantise(raw, on_vector, place=None, held=None):
+            return encode(regroup(raw, on_vector, place), held)
 
         def gather_tokens(g):
             width = GROUP * C
             cols = offs_t[:, g * width // LIST : (g + 1) * width // LIST]
             words = []
             for o in range(PASSES):
-                t = tokp.tile([P, width], U32, name="gw%d" % o, align_bytes=64)
+                t = keep.tile([P, width], U32, name="tok%d_%d" % (g, o), align_bytes=64)
                 nc.vector.tensor_copy(t[:], xw[o][:].bitcast(U32).indirect(cols))
                 words.append(t)
-            sc = tokp.tile([P, width], U8, name="gs", align_bytes=64)
+            sc = keep.tile([P, width], U8, name="tok%d_%d" % (g, PASSES), align_bytes=64)
             nc.vector.tensor_copy(sc[:], xs[:].indirect(cols))
             return words, sc
 
+        def spread_gates():
+            ident = keep.tile([P, P], F32, name="ident")
+            make_identity(nc, ident[:])
+            for i, s in enumerate(parts):
+                depth = (s.stop - s.start) // P
+                cols = keep.tile([P, 2, depth], F32, name="gatecols%d" % i)
+                nc.sync.dma_start(cols[:], gate[:, 0, s].rearrange("r (p c) -> p r c", p=P))
+                for r in range(2):
+                    bank = psum1.tile([P, depth, P], F32, name="sacc%d_%d" % (r, i))
+                    for c in range(depth):
+                        nc.tensor.transpose(bank[:, c, :], cols[:, r, c : c + 1].to_broadcast([P, P]), ident[:])
+                    nc.scalar.copy(
+                        gates[r][:, s].rearrange("n (p c) -> n p c", c=depth), bank[:].rearrange("n c p -> n p c")
+                    )
+
         tokens = {}
 
-        def routed(e, halves, raws, vector_passes):
+        def products(e, accs, weights):
+            if e // GROUP not in tokens:
+                tokens[e // GROUP] = gather_tokens(e // GROUP)
             words, sc = tokens[e // GROUP]
             slots = slice((e % GROUP) * C, (e % GROUP + 1) * C)
-            acc = [psum.tile([P, C], F32, name="acc%d" % h) for h in halves]
-            for o in range(PASSES):
-                grouped = stage.tile([P, len(halves) * P, PACK], BF16, name="grouped", align_bytes=64)
-                cast(raws[o], o in vector_passes, grouped[:])
-                codes, scales = quantise(grouped[:])
-                for i in range(len(halves)):
+            for o, (codes, scales) in enumerate(weights):
+                for i, acc in enumerate(accs):
                     nc.tensor.matmul_mx(
-                        out=acc[i][:],
+                        out=acc,
                         lhsT=codes[:, i * P : (i + 1) * P].bitcast(FP8X4),
                         lhsT_scale=scales[:, i * P : (i + 1) * P],
                         rhs=words[o][:, slots].bitcast(FP8X4),
                         rhs_scale=sc[4 * o : P, slots],
                         start=(o == 0),
-                        stop=(o == PASSES - 1),
+                        stop=(o == LAST),
                     )
-            for i, h in enumerate(halves):
-                nc.scalar.activation(y[h][:, e * C : (e + 1) * C], acc[i][:], GELU, bias=bias[:, h, e : e + 1])
 
-        def load_gates():
-            for r in range(2):
-                nc.sync.dma_start(gates[r][:], gate[r, 0:P, :])
+        def activate(e, h, acc):
+            nc.scalar.activation(y[h][:, e * C : (e + 1) * C], acc, GELU, bias=bias[:, h, e : e + 1])
+
+        def half_phase(h, raws, on_vector, first_place, last_held):
+            batches = [[8, 9, 10], [11]] if h == 0 else [[8, 9, 10], [11]]
+            for n, batch in enumerate(batches):
+                bank = psum.tile([P, len(batch), C], F32, name="acc%d" % (n % 2))
+                for i, e in enumerate(batch):
+                    raw = raws[e - WHOLE]
+                    held = last_held if e == E - 1 else None
+                    if on_vector(e):
+                        weights = quantise(raw[:, :LAST], False) + quantise(raw[:, LAST:], True, held=held)
+                    else:
+                        grouped = regroup(raw, False, first_place if e == WHOLE else None)
+                        weights = encode(grouped[:, :LAST]) + encode(grouped[:, LAST:], held)
+                    products(e, [bank[:, i, :]], weights)
+                for i, e in enumerate(batch):
+                    activate(e, h, bank[:, i, :])
 
         def fetch(h, r, s, name):
             t = keep.tile([P, s.stop - s.start], F32, name=name, align_bytes=64)
@@ -142,69 +185,70 @@ def tile_moe_shr_lin_gelu_kernel(
             )
             return t
 
-        everything = slice(0, N)
         whole = slice(0, T)
-        last = WHOLE * PASSES
-        cuts = [0, 1] + list(range(2, last - 3, PASSES)) + [last - 2, last - 1, last]
-        landed = []
+        spread_gates()
+        nc.sync.dma_start(xw[0][:], x_words[0].rearrange("p t r -> p (t r)").bitcast(I32))
+        first = load_run(0, 1)
+        for o in range(1, PASSES):
+            nc.sync.dma_start(xw[o][:], x_words[o].rearrange("p t r -> p (t r)").bitcast(I32))
+
+        second = load_run(1, 1)
+        nc.sync.dma_start(bias[:], b.rearrange("(h p) e -> p h e", p=P))
+        ahead = quantise(first, False, "tok0_3") + quantise(second, False)
         for e in range(WHOLE):
-            while len(landed) < min((e + 1) * PASSES, last):
-                nxt = cuts[cuts.index(len(landed)) + 1]
-                landed.extend(load_run(len(landed), nxt - len(landed)))
-            raws = landed[e * PASSES : (e + 1) * PASSES]
-            if e == 0:
-                nc.sync.dma_start(bias[:], b.rearrange("(h p) e -> p h e", p=P))
+            raw = load_run(e * PASSES + LAST, PASSES if e + 1 < WHOLE else 1)
+            if e == 2:
                 nc.sync.dma_start(pos[0][:], pos1)
                 nc.sync.dma_start(pos[1][:], pos2)
-            if e % GROUP == 0:
-                tokens[e // GROUP] = gather_tokens(e // GROUP)
-            routed(e, [0, 1], raws, [] if e < SCALAR_ONLY else [2] if e < VECTOR_TWO else [1, 2])
-        for e in range(WHOLE, E):
-            if e % GROUP == 0:
-                tokens[e // GROUP] = gather_tokens(e // GROUP)
-            routed(e, [0], load_passes(e, slice(0, P)), [1, 2])
-        load_gates()
+            place = "tok%d_%d" % (1 + (e + 1) // 4, (e + 1) % 4) if e < 7 else None
+            weights = ahead + quantise(raw[:, :1], True, place)
+            accs = [psum.tile([P, C], F32, name="acc%d" % h) for h in range(HALVES)]
+            products(e, [a[:] for a in accs], weights)
+            if e + 1 < WHOLE:
+                ahead = quantise(raw[:, 1:], False)
+            for h in range(HALVES):
+                activate(e, h, accs[h][:])
+        halves = [[load_passes(e, slice(h * P, (h + 1) * P)) for e in range(WHOLE, E)] for h in range(HALVES)]
+        shared_raw = [load_run(E * PASSES, LAST, "tok1_0"), load_run(E * PASSES + LAST, 1, "tok1_1")]
+        half_phase(0, halves[0], lambda e: True, None, "turn")
+        a0 = fetch(0, 0, whole, "tok0_0")
+        b0 = fetch(0, 1, whole, "tok0_1")
+        nc.vector.tensor_tensor(a0[:], a0[:], b0[:], ADD)
+        shared_grouped = regroup(shared_raw[0], False, "shared0", True)
+        half_phase(1, halves[1], lambda e: e >= E - 1, "turn", "tok1_0")
 
-        parts = [slice(0, 512), slice(512, T)]
         sacc = [
             [psum1.tile([P, s.stop - s.start], F32, name="sacc%d_%d" % (h, i)) for i, s in enumerate(parts)]
             for h in range(HALVES)
         ]
-        raws = load_passes(E, everything)
 
-        def shared_pass(o):
-            grouped = keep.tile([P, N, PACK], BF16, name="hold%d" % o, align_bytes=64)
-            cast(raws[o], False, grouped[:])
-            codes, scales = quantise(grouped[:])
-            for h in range(HALVES):
-                for i, s in enumerate(parts):
-                    nc.tensor.matmul_mx(
-                        out=sacc[h][i][:],
-                        lhsT=codes[:, h * P : (h + 1) * P].bitcast(FP8X4),
-                        lhsT_scale=scales[:, h * P : (h + 1) * P],
-                        rhs=xw[o][:, s].bitcast(FP8X4),
-                        rhs_scale=xs[4 * o : P, s],
-                        start=(o == 0),
-                        stop=(o == PASSES - 1),
-                    )
+        def shared_passes(first, weights):
+            for o, (codes, scales) in enumerate(weights, first):
+                for h in range(HALVES):
+                    for i, s in enumerate(parts):
+                        nc.tensor.matmul_mx(
+                            out=sacc[h][i][:],
+                            lhsT=codes[:, h * P : (h + 1) * P].bitcast(FP8X4),
+                            lhsT_scale=scales[:, h * P : (h + 1) * P],
+                            rhs=xw[o][:, s].bitcast(FP8X4),
+                            rhs_scale=xs[4 * o : P, s],
+                            start=(o == 0),
+                            stop=(o == LAST),
+                        )
 
-        def shared_out():
-            for h in range(HALVES):
-                for i, s in enumerate(parts):
-                    nc.scalar.activation(ys[h][:, s], sacc[h][i][:], GELU, bias=bias[:, h, E : E + 1])
+        shared_passes(0, encode(shared_grouped))
+        shared_passes(LAST, quantise(shared_raw[1], False, "shared1"))
+        for h in range(HALVES):
+            for i, s in enumerate(parts):
+                nc.scalar.activation(ys[h][:, s], sacc[h][i][:], GELU, bias=bias[:, h, E : E + 1])
+        a1 = fetch(1, 0, whole, "tok1_2")
+        left, right = slice(0, T // 2), slice(T // 2, T)
+        b1l = fetch(1, 1, left, "shared1")
 
-        a0 = fetch(0, 0, whole, "a0")
-        b0 = fetch(0, 1, whole, "b0")
-        shared_pass(0)
-        shared_pass(1)
-        a1 = fetch(1, 0, whole, "hold1")
-        shared_pass(2)
-        shared_out()
-        nc.vector.tensor_tensor(a0[:], a0[:], b0[:], ADD)
-        b1 = fetch(1, 1, whole, "hold2")
         nc.vector.tensor_tensor(b0[:], a0[:], ys[0][:], ADD)
         nc.sync.dma_start(out[0:P, :], b0[:])
-        nc.vector.tensor_tensor(a1[:], a1[:], b1[:], ADD)
-        for s in (slice(0, 384), slice(384, T)):
-            nc.vector.tensor_tensor(b1[:, s], a1[:, s], ys[1][:, s], ADD)
-            nc.sync.dma_start(out[P : 2 * P, s], b1[:, s])
+        nc.vector.tensor_tensor(a1[:], a1[:], ys[1][:], ADD)
+        b1r = fetch(1, 1, right, "tok0_2")
+        for s, part in ((left, b1l), (right, b1r)):
+            nc.vector.tensor_tensor(part[:], part[:], a1[:, s], ADD)
+            nc.sync.dma_start(out[P : 2 * P, s], part[:])

from contextlib import ExitStack

import concourse.mybir as mybir
from concourse.masks import make_identity

K, T, E, C, N = 1536, 768, 12, 128, 256
S = E * C
FLOPS = 2 * K * N * (S + T)

F32 = mybir.dt.float32
BF16 = mybir.dt.bfloat16
I32 = mybir.dt.int32
U32 = mybir.dt.uint32
U16 = mybir.dt.uint16
U8 = mybir.dt.uint8
FP8X4 = mybir.dt.float8_e4m3fn_x4
MULT = mybir.AluOpType.mult
ADD = mybir.AluOpType.add
GELU = mybir.ActivationFunctionType.Gelu_apprx_tanh

P = 128
PACK = 4
ROWS = P * PACK
PASSES = K // ROWS
HALVES = N // P
GROUP = 4
LIST = 16
SPLIT = 4
WHOLE = E - SPLIT
BANK = 512
RUN = 4
LAST = PASSES - 1


def tile_moe_shr_lin_gelu_kernel(
    tc, x_words, x_scales, w, b, gate, offs, pos1, pos2, out
):
    nc = tc.nc
    with ExitStack() as ctx:
        keep = ctx.enter_context(tc.tile_pool(name="keep", bufs=1))
        rawp = ctx.enter_context(tc.tile_pool(name="rawp", bufs=9))
        stage = ctx.enter_context(tc.tile_pool(name="stage", bufs=7))
        codep = ctx.enter_context(tc.tile_pool(name="codep", bufs=4))
        psum = ctx.enter_context(tc.psum_pool(name="psum", bufs=2))
        psum1 = ctx.enter_context(tc.psum_pool(name="psum1", bufs=1))

        offs_t = keep.tile([P, S // LIST], U16, name="offs_t")
        nc.sync.dma_start(offs_t[:], offs)
        xs = keep.tile([P, T], U8, name="xs", align_bytes=64)
        nc.gpsimd.memset(xs[:].bitcast(I32), 0)
        for q in range(4):
            nc.scalar.dma_start(
                xs[32 * q : 32 * q + 4 * PASSES, :].bitcast(I32),
                x_scales[:, 4 * q : 4 * q + 4, :].bitcast(I32),
            )
        xw = [keep.tile([P, T], I32, name="xw%d" % o, align_bytes=64) for o in range(PASSES)]
        bias = keep.tile([P, HALVES, E + 1], F32, name="bias")
        pos = [keep.tile([P, T // LIST], U16, name="pos%d" % r) for r in range(2)]
        gates = [keep.tile([P, T], F32, name="gate%d" % r) for r in range(2)]
        y = [keep.tile([P, S], F32, name="y%d" % h) for h in range(HALVES)]
        ys = [keep.tile([P, T], F32, name="ys%d" % h) for h in range(HALVES)]
        parts = [slice(0, BANK), slice(BANK, T)]

        rows = w.rearrange("e (o p j) n -> p (e o) (j n)", p=P, j=PACK)

        def load_run(first, count, place=None):
            if place is None:
                raw = rawp.tile([P, count, PACK * N], F32, name="raw")
            else:
                raw = keep.tile([P, count, PACK * N], F32, name=place, align_bytes=64)
            step = count if place is None else 1
            for i in range(0, count, step):
                nc.sync.dma_start(raw[:, i : i + step, :], rows[:, first + i : first + i + step, :])
            return raw[:].rearrange("p o (j n) -> p o j n", j=PACK)

        def load_passes(e, cols):
            raw = rawp.tile([P, PASSES, PACK, cols.stop - cols.start], F32, name="raw")
            for o in range(PASSES):
                nc.sync.dma_start(
                    raw[:, o, :, :], w[e, o * ROWS : (o + 1) * ROWS, cols].rearrange("(p j) n -> p j n", j=PACK)
                )
            return raw[:]

        def regroup(raw, on_vector, place=None, by_pass=False):
            count, width = raw.shape[1], raw.shape[3]
            if place is None:
                grouped = stage.tile([P, count, width, PACK], BF16, name="grouped", align_bytes=64)
            else:
                grouped = keep.tile([P, count, width, PACK], BF16, name=place, align_bytes=64)
            dst = grouped[:].rearrange("p o (c i) j -> p o c j i", i=RUN)
            src = raw.rearrange("p o j (c i) -> p o c j i", i=RUN)
            if on_vector:
                nc.vector.tensor_copy(dst, src)
            elif by_pass:
                for o in range(count):
                    nc.scalar.copy(dst[:, o], src[:, o])
            else:
                nc.scalar.copy(dst, src)
            return grouped[:]

        def encode(grouped, held=None):
            count, width = grouped.shape[1], grouped.shape[2]
            if held is None:
                codes = codep.tile([P, count * width], U32, name="codes", align_bytes=64)
            else:
                codes = keep.tile([P, count * width], U32, name=held, align_bytes=64)
            scales = codep.tile([P, count * width], U8, name="scales", align_bytes=64)
            nc.vector.quantize_mx(
                out=codes[:].bitcast(FP8X4), scales=scales[:], in_=grouped.rearrange("p o n j -> p (o n j)")
            )
            return [(codes[:, i * width : (i + 1) * width], scales[:, i * width : (i + 1) * width]) for i in range(count)]

        def quantise(raw, on_vector, place=None, held=None):
            return encode(regroup(raw, on_vector, place), held)

        def gather_tokens(g):
            width = GROUP * C
            cols = offs_t[:, g * width // LIST : (g + 1) * width // LIST]
            words = []
            for o in range(PASSES):
                t = keep.tile([P, width], U32, name="tok%d_%d" % (g, o), align_bytes=64)
                nc.vector.tensor_copy(t[:], xw[o][:].bitcast(U32).indirect(cols))
                words.append(t)
            sc = keep.tile([P, width], U8, name="tok%d_%d" % (g, PASSES), align_bytes=64)
            nc.vector.tensor_copy(sc[:], xs[:].indirect(cols))
            return words, sc

        def spread_gates():
            ident = keep.tile([P, P], F32, name="ident")
            make_identity(nc, ident[:])
            for i, s in enumerate(parts):
                depth = (s.stop - s.start) // P
                cols = keep.tile([P, 2, depth], F32, name="gatecols%d" % i)
                nc.sync.dma_start(cols[:], gate[:, 0, s].rearrange("r (p c) -> p r c", p=P))
                for r in range(2):
                    bank = psum1.tile([P, depth, P], F32, name="sacc%d_%d" % (r, i))
                    for c in range(depth):
                        nc.tensor.transpose(bank[:, c, :], cols[:, r, c : c + 1].to_broadcast([P, P]), ident[:])
                    nc.scalar.copy(
                        gates[r][:, s].rearrange("n (p c) -> n p c", c=depth), bank[:].rearrange("n c p -> n p c")
                    )

        tokens = {}

        def products(e, accs, weights):
            if e // GROUP not in tokens:
                tokens[e // GROUP] = gather_tokens(e // GROUP)
            words, sc = tokens[e // GROUP]
            slots = slice((e % GROUP) * C, (e % GROUP + 1) * C)
            for o, (codes, scales) in enumerate(weights):
                for i, acc in enumerate(accs):
                    nc.tensor.matmul_mx(
                        out=acc,
                        lhsT=codes[:, i * P : (i + 1) * P].bitcast(FP8X4),
                        lhsT_scale=scales[:, i * P : (i + 1) * P],
                        rhs=words[o][:, slots].bitcast(FP8X4),
                        rhs_scale=sc[4 * o : P, slots],
                        start=(o == 0),
                        stop=(o == LAST),
                    )

        def activate(e, h, acc):
            nc.scalar.activation(y[h][:, e * C : (e + 1) * C], acc, GELU, bias=bias[:, h, e : e + 1])

        def half_phase(h, raws, on_vector, first_place, last_held):
            batches = [[8, 9, 10], [11]] if h == 0 else [[8, 9, 10], [11]]
            for n, batch in enumerate(batches):
                bank = psum.tile([P, len(batch), C], F32, name="acc%d" % (n % 2))
                for i, e in enumerate(batch):
                    raw = raws[e - WHOLE]
                    held = last_held if e == E - 1 else None
                    if on_vector(e):
                        weights = quantise(raw[:, :LAST], False) + quantise(raw[:, LAST:], True, held=held)
                    else:
                        grouped = regroup(raw, False, first_place if e == WHOLE else None)
                        weights = encode(grouped[:, :LAST]) + encode(grouped[:, LAST:], held)
                    products(e, [bank[:, i, :]], weights)
                for i, e in enumerate(batch):
                    activate(e, h, bank[:, i, :])

        def fetch(h, r, s, name):
            t = keep.tile([P, s.stop - s.start], F32, name=name, align_bytes=64)
            nc.vector.tensor_tensor(
                t[:], y[h][:].indirect(pos[r][:, s.start // LIST : s.stop // LIST]), gates[r][:, s], MULT
            )
            return t

        whole = slice(0, T)
        spread_gates()
        nc.sync.dma_start(xw[0][:], x_words[0].rearrange("p t r -> p (t r)").bitcast(I32))
        first = load_run(0, 1)
        for o in range(1, PASSES):
            nc.sync.dma_start(xw[o][:], x_words[o].rearrange("p t r -> p (t r)").bitcast(I32))

        second = load_run(1, 1)
        nc.sync.dma_start(bias[:], b.rearrange("(h p) e -> p h e", p=P))
        ahead = quantise(first, False, "tok0_3") + quantise(second, False)
        for e in range(WHOLE):
            raw = load_run(e * PASSES + LAST, PASSES if e + 1 < WHOLE else 1)
            if e == 2:
                nc.sync.dma_start(pos[0][:], pos1)
                nc.sync.dma_start(pos[1][:], pos2)
            place = "tok%d_%d" % (1 + (e + 1) // 4, (e + 1) % 4) if e < 7 else None
            weights = ahead + quantise(raw[:, :1], True, place)
            accs = [psum.tile([P, C], F32, name="acc%d" % h) for h in range(HALVES)]
            products(e, [a[:] for a in accs], weights)
            if e + 1 < WHOLE:
                ahead = quantise(raw[:, 1:], False)
            for h in range(HALVES):
                activate(e, h, accs[h][:])
        halves = [[load_passes(e, slice(h * P, (h + 1) * P)) for e in range(WHOLE, E)] for h in range(HALVES)]
        shared_raw = [load_run(E * PASSES, LAST, "tok1_0"), load_run(E * PASSES + LAST, 1, "tok1_1")]
        half_phase(0, halves[0], lambda e: True, None, "turn")
        a0 = fetch(0, 0, whole, "tok0_0")
        b0 = fetch(0, 1, whole, "tok0_1")
        nc.vector.tensor_tensor(a0[:], a0[:], b0[:], ADD)
        shared_grouped = regroup(shared_raw[0], False, "shared0", True)
        half_phase(1, halves[1], lambda e: e >= E - 1, "turn", "tok1_0")

        sacc = [
            [psum1.tile([P, s.stop - s.start], F32, name="sacc%d_%d" % (h, i)) for i, s in enumerate(parts)]
            for h in range(HALVES)
        ]

        def shared_passes(first, weights):
            for o, (codes, scales) in enumerate(weights, first):
                for h in range(HALVES):
                    for i, s in enumerate(parts):
                        nc.tensor.matmul_mx(
                            out=sacc[h][i][:],
                            lhsT=codes[:, h * P : (h + 1) * P].bitcast(FP8X4),
                            lhsT_scale=scales[:, h * P : (h + 1) * P],
                            rhs=xw[o][:, s].bitcast(FP8X4),
                            rhs_scale=xs[4 * o : P, s],
                            start=(o == 0),
                            stop=(o == LAST),
                        )

        shared_passes(0, encode(shared_grouped))
        shared_passes(LAST, quantise(shared_raw[1], False, "shared1"))
        for h in range(HALVES):
            for i, s in enumerate(parts):
                nc.scalar.activation(ys[h][:, s], sacc[h][i][:], GELU, bias=bias[:, h, E : E + 1])
        a1 = fetch(1, 0, whole, "tok1_2")
        left, right = slice(0, T // 2), slice(T // 2, T)
        b1l = fetch(1, 1, left, "shared1")

        nc.vector.tensor_tensor(b0[:], a0[:], ys[0][:], ADD)
        nc.sync.dma_start(out[0:P, :], b0[:])
        nc.vector.tensor_tensor(a1[:], a1[:], ys[1][:], ADD)
        b1r = fetch(1, 1, right, "tok0_2")
        for s, part in ((left, b1l), (right, b1r)):
            nc.vector.tensor_tensor(part[:], part[:], a1[:, s], ADD)
            nc.sync.dma_start(out[P : 2 * P, s], part[:])
